import numpy as np
import ml_dtypes

BF16 = ml_dtypes.bfloat16


def bf(x):
    return np.asarray(x, np.float32).astype(BF16)


def f32(x):
    return np.asarray(x, np.float32)


def f64(x):
    return np.asarray(x).astype(np.float64)


def striped(idx):
    return np.tile(idx.reshape(-1, 16).T, (8, 1))


def rows(idx, k):
    return np.tile(idx, (k, 1))


def look(tab, idx):
    return np.take_along_axis(f64(tab), rows(idx, len(tab)), axis=1)


K, S, V, N = 128, 2048, 512, 512


def silu(v):
    return v / (1.0 + np.exp(-v))


def setup_inputs():
    return {"tab": f32(np.random.standard_normal((2, K, S))), "y": f32(np.random.standard_normal((K, V))), "offs": striped(np.random.permutation(S)[:N])}


def reference(tab, y, offs):
    idx = offs[:16].T.reshape(-1)
    x = (np.minimum(look(tab[0], idx), f64(y))) * (silu(look(tab[1], idx)))
    return x

@@ -1,0 +1,33 @@
+import concourse.mybir as mybir
+
+F32 = mybir.dt.float32
+U16 = mybir.dt.uint16
+MIN = mybir.AluOpType.min
+MULT = mybir.AluOpType.mult
+SILU = mybir.ActivationFunctionType.Silu
+
+ROWS, PLACES, PICKS = 128, 2048, 512
+
+FLOPS = 6 * ROWS * PICKS
+
+
+def tile_lookup_vg_minsilu_out_kernel(tc, tab, y, offs, out):
+    nc = tc.nc
+    with tc.tile_pool(name="held", bufs=1) as held:
+        offsets = held.tile([ROWS, PICKS // 16], U16, name="offsets")
+        gates = held.tile([ROWS, PLACES], F32, name="gates")
+        values = held.tile([ROWS, PLACES], F32, name="values")
+        stream = held.tile([ROWS, PICKS], F32, name="stream")
+        gated = held.tile([ROWS, PICKS], F32, name="gated")
+        lesser = held.tile([ROWS, PICKS], F32, name="lesser")
+        product = held.tile([ROWS, PICKS], F32, name="product")
+
+        nc.sync.dma_start(offsets[:], offs)
+        nc.sync.dma_start(gates[:], tab[1])
+        nc.sync.dma_start(stream[:], y)
+        nc.sync.dma_start(values[:], tab[0])
+
+        nc.scalar.activation(gated[:], gates[:].indirect(offsets[:]), SILU)
+        nc.vector.tensor_tensor(lesser[:], values[:].indirect(offsets[:]), stream[:], MIN)
+        nc.vector.tensor_tensor(product[:], lesser[:], gated[:], MULT)
+        nc.sync.dma_start(out, product[:])

@@ -8,6 +8,8 @@ SILU = mybir.ActivationFunctionType.Silu
 
 ROWS, PLACES, PICKS = 128, 2048, 512
 
+PIECE = PICKS // 2
+
 FLOPS = 6 * ROWS * PICKS
 
 
@@ -28,6 +30,9 @@ def tile_lookup_vg_minsilu_out_kernel(tc, tab, y, offs, out):
         nc.sync.dma_start(values[:], tab[0])
 
         nc.scalar.activation(gated[:], gates[:].indirect(offsets[:]), SILU)
-        nc.vector.tensor_tensor(lesser[:], values[:].indirect(offsets[:]), stream[:], MIN)
-        nc.vector.tensor_tensor(product[:], lesser[:], gated[:], MULT)
-        nc.sync.dma_start(out, product[:])
+        for first in range(0, PICKS, PIECE):
+            piece = slice(first, first + PIECE)
+            piece_offsets = offsets[:, first // 16 : (first + PIECE) // 16]
+            nc.vector.tensor_tensor(lesser[:, piece], values[:].indirect(piece_offsets), stream[:, piece], MIN)
+            nc.vector.tensor_tensor(product[:, piece], lesser[:, piece], gated[:, piece], MULT)
+            nc.sync.dma_start(out[:, piece], product[:, piece])

@@ -24,6 +24,11 @@ def tile_lookup_vg_minsilu_out_kernel(tc, tab, y, offs, out):
         lesser = held.tile([ROWS, PICKS], F32, name="lesser")
         product = held.tile([ROWS, PICKS], F32, name="product")
 
+        zeros = held.tile([ROWS, 1], F32, name="zeros")
+        warmed = held.tile([ROWS, 1], F32, name="warmed")
+        nc.vector.memset(zeros[:], 0.0)
+        nc.scalar.activation(warmed[:], zeros[:], SILU)
+
         nc.sync.dma_start(offsets[:], offs)
         nc.sync.dma_start(gates[:], tab[1])
         nc.sync.dma_start(stream[:], y)

import concourse.mybir as mybir

F32 = mybir.dt.float32
U16 = mybir.dt.uint16
MIN = mybir.AluOpType.min
MULT = mybir.AluOpType.mult
SILU = mybir.ActivationFunctionType.Silu

ROWS, PLACES, PICKS = 128, 2048, 512

PIECE = PICKS // 2

FLOPS = 6 * ROWS * PICKS


def tile_lookup_vg_minsilu_out_kernel(tc, tab, y, offs, out):
    nc = tc.nc
    with tc.tile_pool(name="held", bufs=1) as held:
        offsets = held.tile([ROWS, PICKS // 16], U16, name="offsets")
        gates = held.tile([ROWS, PLACES], F32, name="gates")
        values = held.tile([ROWS, PLACES], F32, name="values")
        stream = held.tile([ROWS, PICKS], F32, name="stream")
        gated = held.tile([ROWS, PICKS], F32, name="gated")
        lesser = held.tile([ROWS, PICKS], F32, name="lesser")
        product = held.tile([ROWS, PICKS], F32, name="product")

        zeros = held.tile([ROWS, 1], F32, name="zeros")
        warmed = held.tile([ROWS, 1], F32, name="warmed")
        nc.vector.memset(zeros[:], 0.0)
        nc.scalar.activation(warmed[:], zeros[:], SILU)

        nc.sync.dma_start(offsets[:], offs)
        nc.sync.dma_start(gates[:], tab[1])
        nc.sync.dma_start(stream[:], y)
        nc.sync.dma_start(values[:], tab[0])

        nc.scalar.activation(gated[:], gates[:].indirect(offsets[:]), SILU)
        for first in range(0, PICKS, PIECE):
            piece = slice(first, first + PIECE)
            piece_offsets = offsets[:, first // 16 : (first + PIECE) // 16]
            nc.vector.tensor_tensor(lesser[:, piece], values[:].indirect(piece_offsets), stream[:, piece], MIN)
            nc.vector.tensor_tensor(product[:, piece], lesser[:, piece], gated[:, piece], MULT)
            nc.sync.dma_start(out[:, piece], product[:, piece])
